import numpy as np
import ml_dtypes


def mxq(x, axis, fmt="e4m3"):
    dtype, down = {"e4m3": (ml_dtypes.float8_e4m3fn, 7), "e5m2": (ml_dtypes.float8_e5m2, 14)}[fmt]
    v = np.moveaxis(np.asarray(x, np.float32).astype(ml_dtypes.bfloat16).astype(np.float64), axis, -1)
    blocks = v.reshape(v.shape[:-1] + (-1, 32))
    amax = np.abs(blocks).max(-1, keepdims=True)
    byte = np.maximum(np.where(amax > 0, np.frexp(amax)[1] - 1 + 127, 0) - down, 1)
    scale = np.exp2(byte - 127.0)
    codes = (blocks / scale).astype(np.float32).astype(dtype).astype(np.float64)
    return np.moveaxis((codes * scale).reshape(v.shape), -1, axis)


WIDE = False


def mx_kscale(k):
    if not WIDE:
        return np.ones(k)
    levels = np.array([10, -10, 5, -5, 0])
    if k % 512:
        return np.exp2(np.random.permutation(np.resize(levels, k // 32))).repeat(32)
    a = np.empty((k // 512, 16))
    for p in range(k // 512):
        a[p, :8] = np.random.permutation(np.resize(levels, 8))
        for g in range(8):
            far = levels[np.abs(levels - a[p, g]) >= 10]
            a[p, g + 8] = far[np.random.randint(len(far))]
    return np.exp2(a.ravel()).repeat(32)


def f64(x):
    return np.asarray(x).astype(np.float64)


def striped(idx):
    return np.tile(idx.reshape(-1, 16).T, (8, 1)).astype(np.uint16)


def unstriped(offs):
    return offs[:16].T.reshape(-1).astype(np.int64)


K, T, E, C, N = 1536, 1024, 16, 128, 128


def by_expert(wq, xq):
    return np.concatenate([wq[e].T @ xq[:, e * C:(e + 1) * C] for e in range(E)], axis=1)


def setup_inputs():
    n = np.random.standard_normal
    s = mx_kscale(K)[:, None]
    first = np.random.permutation(np.repeat(np.arange(E), T // E))
    second = (first + 1 + np.random.permutation(np.repeat(np.arange(E - 1), -(-T // (E - 1)))[:T])) % E
    while np.bincount(second, minlength=E).max() != T // E:
        load = np.bincount(second, minlength=E); hi, lo = int(load.argmax()), int(load.argmin())
        t = np.flatnonzero((second == hi) & (first != lo))[0]; second[t] = lo
    slot_token = np.empty(E * C, np.int64); pos = np.empty((2, T), np.int64); fill = np.zeros(E, np.int64)
    place = np.stack([np.random.permutation(C) for _ in range(E)])
    for r, deal in enumerate((first, second)):
        for t in np.random.permutation(T):
            e = deal[t]; j = e * C + place[e, fill[e]]; fill[e] += 1; slot_token[j] = t; pos[r, t] = j
    g = np.random.uniform(0.2, 0.8, T)
    return {
        "xT": (n((K, T)) * s).astype(np.float32),
        "w": (n((E, K, N)) / np.sqrt(K) / s[None]).astype(np.float32),
        "gate": np.stack([np.tile(g, (N, 1)), np.tile(1.0 - g, (N, 1))]).astype(np.float32),
        "offs": striped(slot_token),
        "pos1": striped(pos[0]),
        "pos2": striped(pos[1]),
    }


def reference(xT, w, gate, offs, pos1, pos2):
    idx = unstriped(offs)
    xq = mxq(f64(xT)[:, idx], 0, "e4m3")
    y = by_expert(mxq(f64(w), 1, "e4m3"), xq)
    return f64(gate[0]) * y[:, unstriped(pos1)] + f64(gate[1]) * y[:, unstriped(pos2)]

@@ -1,0 +1,223 @@
+from contextlib import ExitStack
+
+import concourse.mybir as mybir
+
+K, T, E, C, N = 1536, 1024, 16, 128, 128
+FLOPS = 2 * K * E * C * N
+
+F32 = mybir.dt.float32
+BF16 = mybir.dt.bfloat16
+U32 = mybir.dt.uint32
+U16 = mybir.dt.uint16
+U8 = mybir.dt.uint8
+FP8X4 = mybir.dt.float8_e4m3fn_x4
+MULT = mybir.AluOpType.mult
+
+P = 128
+PACK = 4
+PASSES = K // (P * PACK)
+SLOTS = E * C
+AHEAD = 11
+
+X_UNITS = [
+    (0, 0, 256, 128), (0, 256, 256, 128), (0, 512, 512, 192),
+    (1, 0, 512, 192), (1, 512, 512, 192),
+    (2, 0, 512, 192), (2, 512, 512, 192),
+]
+W_SIZES = [(4, 0), (4, 1), (4, 0), (4, 1), (4, 0), (4, 1), (4, 0), (4, 1), (4, 0), (4, 1), (4, 1), (2, 1), (1, 0), (1, 1)]
+SLOT_CUTS = [(0, 768), (768, 1408), (1408, 2048)]
+BANKS = [(0, 4), (4, 8), (8, 12), (12, 14), (14, 15), (15, 16)]
+
+
+def by_fours(grouped, raw):
+    return grouped.rearrange("p (c i) t -> p c t i", i=4), raw.rearrange("p t (c i) -> p c t i", i=4)
+
+
+def by_fours_w(grouped, raw):
+    return grouped.rearrange("p g (c i) t -> p g c t i", i=4), raw.rearrange("p g t (c i) -> p g c t i", i=4)
+
+
+def tile_routed_moe_kernel(tc, xT, w, gate, offs, pos1, pos2, out):
+    nc = tc.nc
+    x_rows = xT.rearrange("(a p t) n -> a p t n", p=P, t=PACK)
+    w_rows = w.flatten_outer_dims().rearrange("(g p t) n -> p g t n", p=P, t=PACK)
+
+    with ExitStack() as ctx:
+        keep = ctx.enter_context(tc.tile_pool(name="keep", bufs=1))
+        raws = ctx.enter_context(tc.tile_pool(name="raws", bufs=12))
+        mids = ctx.enter_context(tc.tile_pool(name="mids", bufs=6))
+        psum = ctx.enter_context(tc.psum_pool(name="psum", bufs=1))
+
+        offs_sb = keep.tile([P, SLOTS // 16], U16, name="offs_sb")
+        pos1_sb = keep.tile([P, T // 16], U16, name="pos1_sb")
+        pos2_sb = keep.tile([P, T // 16], U16, name="pos2_sb")
+
+        x_codes = [keep.tile([P, T], U32, name=f"x_codes{a}", align_bytes=64) for a in range(PASSES)]
+        x_scales = keep.tile([P, T], U8, name="x_scales", align_bytes=64)
+        s_codes = [keep.tile([P, SLOTS], U32, name=f"s_codes{a}", align_bytes=64) for a in range(PASSES)]
+        s_scales = keep.tile([P, SLOTS], U8, name="s_scales", align_bytes=64)
+        w_codes = keep.tile([P, E * PASSES * N], U32, name="w_codes", align_bytes=64)
+        w_scales = keep.tile([P, E * PASSES * N], U8, name="w_scales", align_bytes=64)
+        gates = keep.tile([P, 2, T], F32, name="gates")
+        y = keep.tile([P, SLOTS], F32, name="y")
+        first = keep.tile([P, T], F32, name="first")
+        second = keep.tile([P, T], F32, name="second")
+        total = keep.tile([P, T], F32, name="total")
+        warm = keep.tile([P, 8], F32, name="warm")
+
+        nc.gpsimd.memset(x_scales[:], 0)
+        nc.vector.memset(warm[:], 0.0)
+        nc.scalar.copy(warm[:, 4:8], warm[:, 0:4])
+
+        units = [("x",) + u for u in X_UNITS]
+        g0 = 0
+        for size, on_vector in W_SIZES:
+            units.append(("w", g0, size, on_vector))
+            g0 += size
+        raw_of = {}
+        mid_of = {}
+
+        def load(u):
+            if u >= len(units):
+                return
+            unit = units[u]
+            if unit[0] == "x":
+                kind, a, c0, n, on_vector = unit
+                raw = raws.tile([P, PACK, n], F32, name="raw", tag="raw", align_bytes=64)
+                nc.sync.dma_start(out=raw[:], in_=x_rows[a, :, :, c0:c0 + n])
+            else:
+                kind, g, n, on_vector = unit
+                raw = raws.tile([P, n, PACK, N], F32, name="raw", tag="raw", align_bytes=64)
+                nc.sync.dma_start(out=raw[:], in_=w_rows[:, g:g + n, :, :])
+            raw_of[u] = raw
+            if u == 1:
+                nc.sync.dma_start(offs_sb[:], offs)
+            if u == len(units) - 5:
+                nc.sync.dma_start(pos1_sb[:], pos1)
+                nc.sync.dma_start(pos2_sb[:], pos2)
+            if u == len(units) - 1:
+                for r in range(2):
+                    nc.sync.dma_start(out=gates[:, r, :], in_=gate[r])
+
+        def interleave(u):
+            unit = units[u]
+            raw = raw_of[u]
+            if unit[0] == "x":
+                kind, a, c0, n, cut = unit
+                mid = mids.tile([P, n, PACK], BF16, name="mid", tag="mid", align_bytes=64)
+                dst, src = by_fours(mid[:, 0:cut, :], raw[:, :, 0:cut])
+                nc.vector.tensor_copy(dst, src)
+                dst, src = by_fours(mid[:, cut:n, :], raw[:, :, cut:n])
+                nc.scalar.copy(dst, src)
+            else:
+                kind, g, n, cut = unit
+                mid = mids.tile([P, n, N, PACK], BF16, name="mid", tag="mid", align_bytes=64)
+                if cut > 0:
+                    dst, src = by_fours_w(mid[:, n - cut:n], raw[:, n - cut:n])
+                    nc.vector.tensor_copy(dst, src)
+                if cut < n:
+                    dst, src = by_fours_w(mid[:, 0:n - cut], raw[:, 0:n - cut])
+                    nc.scalar.copy(dst, src)
+            mid_of[u] = mid
+
+        def quantize(u):
+            unit = units[u]
+            mid = mid_of[u]
+            if unit[0] == "x":
+                kind, a, c0, n, cut = unit
+                nc.vector.quantize_mx(
+                    out=x_codes[a][:, c0:c0 + n].bitcast(FP8X4),
+                    scales=x_scales[4 * a:P, c0:c0 + n],
+                    in_=mid[:].rearrange("p n t -> p (n t)"),
+                )
+            else:
+                kind, g, n, cut = unit
+                cols = slice(g * N, (g + n) * N)
+                nc.vector.quantize_mx(
+                    out=w_codes[:, cols].bitcast(FP8X4),
+                    scales=w_scales[:, cols],
+                    in_=mid[:].rearrange("p g n t -> p (g n t)"),
+                )
+
+        def gather_words(a, lo, hi):
+            nc.vector.tensor_copy(s_codes[a][:, lo:hi], x_codes[a][:].indirect(offs_sb[:, lo // 16:hi // 16]))
+
+        def gather_bytes(lo, hi):
+            nc.vector.tensor_copy(s_scales[:, lo:hi], x_scales[:].indirect(offs_sb[:, lo // 16:hi // 16]))
+
+        bank_of = {}
+
+        def multiply(e):
+            for b, (e0, e1) in enumerate(BANKS):
+                if e0 <= e < e1:
+                    break
+            if e == e0:
+                bank_of[b] = psum.tile([P, (e1 - e0) * C], F32, name=f"bank{b}")
+            bank = bank_of[b]
+            for a in range(PASSES):
+                wc = slice((e * PASSES + a) * N, (e * PASSES + a + 1) * N)
+                sc = slice(e * C, (e + 1) * C)
+                nc.tensor.matmul_mx(
+                    out=bank[:, (e - e0) * C:(e - e0 + 1) * C],
+                    lhsT=w_codes[:, wc].bitcast(FP8X4),
+                    lhsT_scale=w_scales[:, wc],
+                    rhs=s_codes[a][:, sc].bitcast(FP8X4),
+                    rhs_scale=s_scales[4 * a:P, sc],
+                    start=(a == 0),
+                    stop=(a == PASSES - 1),
+                )
+            if e == e1 - 1:
+                if e1 == E:
+                    nc.vector.tensor_copy(y[:, e0 * C:e1 * C], bank[:])
+                else:
+                    nc.scalar.copy(y[:, e0 * C:e1 * C], bank[:])
+
+        jobs = []
+        done = 0
+
+        def after(u, done):
+            unit = units[u]
+            if unit[0] == "x":
+                a, last = unit[1], unit[2] + unit[3] == T
+                if last and a < PASSES - 1:
+                    jobs.extend([(gather_words, (a, lo, hi)) for lo, hi in SLOT_CUTS])
+                if last and a == PASSES - 1:
+                    for lo, hi in SLOT_CUTS:
+                        jobs.append((gather_words, (a, lo, hi)))
+                        jobs.append((gather_bytes, (lo, hi)))
+            for i in range(2):
+                if jobs:
+                    f, args = jobs.pop(0)
+                    f(*args)
+            if unit[0] == "w" and not jobs:
+                while done < E and (done + 1) * PASSES <= unit[1] + unit[2]:
+                    multiply(done)
+                    done += 1
+            return done
+
+        for u in range(AHEAD):
+            load(u)
+        for u in range(len(units) + 1):
+            if u < len(units):
+                interleave(u)
+            load(u + AHEAD)
+            if u > 0:
+                quantize(u - 1)
+                done = after(u - 1, done)
+
+        def fetch(dst, r, lo, hi):
+            pos = pos1_sb if r == 0 else pos2_sb
+            nc.vector.tensor_tensor(dst[:, lo:hi], y[:].indirect(pos[:, lo // 16:hi // 16]), gates[:, r, lo:hi], MULT)
+
+        def finish(lo, hi):
+            nc.vector.tensor_add(total[:, lo:hi], first[:, lo:hi], second[:, lo:hi])
+            nc.sync.dma_start(out=out[:, lo:hi], in_=total[:, lo:hi])
+
+        fetch(first, 0, 0, 512)
+        fetch(first, 0, 512, 1024)
+        fetch(second, 1, 0, 512)
+        finish(0, 512)
+        fetch(second, 1, 512, 768)
+        finish(512, 768)
+        fetch(second, 1, 768, 1024)
+        finish(768, 1024)

@@ -17,14 +17,14 @@ P = 128
 PACK = 4
 PASSES = K // (P * PACK)
 SLOTS = E * C
-AHEAD = 11
+AHEAD = 6
 
 X_UNITS = [
-    (0, 0, 256, 128), (0, 256, 256, 128), (0, 512, 512, 192),
-    (1, 0, 512, 192), (1, 512, 512, 192),
-    (2, 0, 512, 192), (2, 512, 512, 192),
+    (0, 0, 256, 256), (0, 256, 256, 256), (0, 512, 512, 384),
+    (1, 0, 512, 0), (1, 512, 512, 0),
+    (2, 0, 512, 0), (2, 512, 512, 0),
 ]
-W_SIZES = [(4, 0), (4, 1), (4, 0), (4, 1), (4, 0), (4, 1), (4, 0), (4, 1), (4, 0), (4, 1), (4, 1), (2, 1), (1, 0), (1, 1)]
+W_SIZES = [(4, 0, 1)] * 7 + [(4, 2, 0), (4, 2, 0), (4, 2, 0), (4, 2, 0), (2, 1, 0), (1, 0, 0), (1, 1, 0)]
 SLOT_CUTS = [(0, 768), (768, 1408), (1408, 2048)]
 BANKS = [(0, 4), (4, 8), (8, 12), (12, 14), (14, 15), (15, 16)]
 
@@ -44,8 +44,8 @@ def tile_routed_moe_kernel(tc, xT, w, gate, offs, pos1, pos2, out):
 
     with ExitStack() as ctx:
         keep = ctx.enter_context(tc.tile_pool(name="keep", bufs=1))
-        raws = ctx.enter_context(tc.tile_pool(name="raws", bufs=12))
-        mids = ctx.enter_context(tc.tile_pool(name="mids", bufs=6))
+        raws = ctx.enter_context(tc.tile_pool(name="raws", bufs=7))
+        mids = ctx.enter_context(tc.tile_pool(name="mids", bufs=20))
         psum = ctx.enter_context(tc.psum_pool(name="psum", bufs=1))
 
         offs_sb = keep.tile([P, SLOTS // 16], U16, name="offs_sb")
@@ -62,7 +62,6 @@ def tile_routed_moe_kernel(tc, xT, w, gate, offs, pos1, pos2, out):
         y = keep.tile([P, SLOTS], F32, name="y")
         first = keep.tile([P, T], F32, name="first")
         second = keep.tile([P, T], F32, name="second")
-        total = keep.tile([P, T], F32, name="total")
         warm = keep.tile([P, 8], F32, name="warm")
 
         nc.gpsimd.memset(x_scales[:], 0)
@@ -71,8 +70,8 @@ def tile_routed_moe_kernel(tc, xT, w, gate, offs, pos1, pos2, out):
 
         units = [("x",) + u for u in X_UNITS]
         g0 = 0
-        for size, on_vector in W_SIZES:
-            units.append(("w", g0, size, on_vector))
+        for size, on_vector, on_gpsimd in W_SIZES:
+            units.append(("w", g0, size, on_vector, on_gpsimd))
             g0 += size
         raw_of = {}
         mid_of = {}
@@ -86,7 +85,7 @@ def tile_routed_moe_kernel(tc, xT, w, gate, offs, pos1, pos2, out):
                 raw = raws.tile([P, PACK, n], F32, name="raw", tag="raw", align_bytes=64)
                 nc.sync.dma_start(out=raw[:], in_=x_rows[a, :, :, c0:c0 + n])
             else:
-                kind, g, n, on_vector = unit
+                kind, g, n, on_vector, on_gpsimd = unit
                 raw = raws.tile([P, n, PACK, N], F32, name="raw", tag="raw", align_bytes=64)
                 nc.sync.dma_start(out=raw[:], in_=w_rows[:, g:g + n, :, :])
             raw_of[u] = raw
@@ -105,18 +104,23 @@ def tile_routed_moe_kernel(tc, xT, w, gate, offs, pos1, pos2, out):
             if unit[0] == "x":
                 kind, a, c0, n, cut = unit
                 mid = mids.tile([P, n, PACK], BF16, name="mid", tag="mid", align_bytes=64)
-                dst, src = by_fours(mid[:, 0:cut, :], raw[:, :, 0:cut])
-                nc.vector.tensor_copy(dst, src)
-                dst, src = by_fours(mid[:, cut:n, :], raw[:, :, cut:n])
-                nc.scalar.copy(dst, src)
+                if cut > 0:
+                    dst, src = by_fours(mid[:, 0:cut, :], raw[:, :, 0:cut])
+                    nc.vector.tensor_copy(dst, src)
+                if cut < n:
+                    dst, src = by_fours(mid[:, cut:n, :], raw[:, :, cut:n])
+                    nc.scalar.copy(dst, src)
             else:
-                kind, g, n, cut = unit
+                kind, g, n, cut, head = unit
                 mid = mids.tile([P, n, N, PACK], BF16, name="mid", tag="mid", align_bytes=64)
                 if cut > 0:
                     dst, src = by_fours_w(mid[:, n - cut:n], raw[:, n - cut:n])
                     nc.vector.tensor_copy(dst, src)
-                if cut < n:
-                    dst, src = by_fours_w(mid[:, 0:n - cut], raw[:, 0:n - cut])
+                if head > 0:
+                    dst, src = by_fours_w(mid[:, 0:head], raw[:, 0:head])
+                    nc.gpsimd.tensor_copy(dst, src)
+                if head < n - cut:
+                    dst, src = by_fours_w(mid[:, head:n - cut], raw[:, head:n - cut])
                     nc.scalar.copy(dst, src)
             mid_of[u] = mid
 
@@ -131,7 +135,7 @@ def tile_routed_moe_kernel(tc, xT, w, gate, offs, pos1, pos2, out):
                     in_=mid[:].rearrange("p n t -> p (n t)"),
                 )
             else:
-                kind, g, n, cut = unit
+                kind, g, n, cut, head = unit
                 cols = slice(g * N, (g + n) * N)
                 nc.vector.quantize_mx(
                     out=w_codes[:, cols].bitcast(FP8X4),
@@ -185,7 +189,7 @@ def tile_routed_moe_kernel(tc, xT, w, gate, offs, pos1, pos2, out):
                     for lo, hi in SLOT_CUTS:
                         jobs.append((gather_words, (a, lo, hi)))
                         jobs.append((gather_bytes, (lo, hi)))
-            for i in range(2):
+            for i in range(1):
                 if jobs:
                     f, args = jobs.pop(0)
                     f(*args)
@@ -210,14 +214,14 @@ def tile_routed_moe_kernel(tc, xT, w, gate, offs, pos1, pos2, out):
             nc.vector.tensor_tensor(dst[:, lo:hi], y[:].indirect(pos[:, lo // 16:hi // 16]), gates[:, r, lo:hi], MULT)
 
         def finish(lo, hi):
-            nc.vector.tensor_add(total[:, lo:hi], first[:, lo:hi], second[:, lo:hi])
-            nc.sync.dma_start(out=out[:, lo:hi], in_=total[:, lo:hi])
+            nc.vector.tensor_add(first[:, lo:hi], first[:, lo:hi], second[:, lo:hi])
+            nc.sync.dma_start(out=out[:, lo:hi], in_=first[:, lo:hi])
 
         fetch(first, 0, 0, 512)
         fetch(first, 0, 512, 1024)
         fetch(second, 1, 0, 512)
         finish(0, 512)
-        fetch(second, 1, 512, 768)
-        finish(512, 768)
-        fetch(second, 1, 768, 1024)
-        finish(768, 1024)
+        fetch(second, 1, 512, 896)
+        finish(512, 896)
+        fetch(second, 1, 896, 1024)
+        finish(896, 1024)

@@ -17,35 +17,32 @@ P = 128
 PACK = 4
 PASSES = K // (P * PACK)
 SLOTS = E * C
-AHEAD = 6
+AHEAD = 7
+
 
 X_UNITS = [
-    (0, 0, 256, 256), (0, 256, 256, 256), (0, 512, 512, 384),
-    (1, 0, 512, 0), (1, 512, 512, 0),
-    (2, 0, 512, 0), (2, 512, 512, 0),
+    (0, 0, [(512, [("V", 512)])]), (0, 512, [(256, [("S", 256)]), (256, [("V", 256)])]),
+    (1, 0, [(512, [("S", 512)])]), (1, 512, [(512, [("S", 512)])]),
+    (2, 0, [(512, [("S", 512)])]), (2, 512, [(512, [("S", 512)])]),
 ]
-W_SIZES = [(4, 0, 1)] * 7 + [(4, 2, 0), (4, 2, 0), (4, 2, 0), (4, 2, 0), (2, 1, 0), (1, 0, 0), (1, 1, 0)]
+W_UNITS = [[(4, [("S", 4)]), (4, [("G", 2), ("S", 2)])]] * 3 + [[(4, [("G", 1), ("S", 3)]), (4, [("G", 2), ("S", 2)])]] * 2 + [
+    [(4, [("G", 1), ("S", 3)])], [(2, [("S", 2)])], [(2, [("S", 1), ("V", 1)])]]
 SLOT_CUTS = [(0, 768), (768, 1408), (1408, 2048)]
-BANKS = [(0, 4), (4, 8), (8, 12), (12, 14), (14, 15), (15, 16)]
-
-
-def by_fours(grouped, raw):
-    return grouped.rearrange("p (c i) t -> p c t i", i=4), raw.rearrange("p t (c i) -> p c t i", i=4)
-
-
-def by_fours_w(grouped, raw):
-    return grouped.rearrange("p g (c i) t -> p g c t i", i=4), raw.rearrange("p g t (c i) -> p g c t i", i=4)
+BANKS = [(0, 4), (4, 8), (8, 12), (12, 15), (15, 16)]
 
 
 def tile_routed_moe_kernel(tc, xT, w, gate, offs, pos1, pos2, out):
     nc = tc.nc
     x_rows = xT.rearrange("(a p t) n -> a p t n", p=P, t=PACK)
     w_rows = w.flatten_outer_dims().rearrange("(g p t) n -> p g t n", p=P, t=PACK)
+    move = {"V": nc.vector.tensor_copy, "S": nc.scalar.copy, "G": nc.gpsimd.tensor_copy}
 
     with ExitStack() as ctx:
         keep = ctx.enter_context(tc.tile_pool(name="keep", bufs=1))
-        raws = ctx.enter_context(tc.tile_pool(name="raws", bufs=7))
-        mids = ctx.enter_context(tc.tile_pool(name="mids", bufs=20))
+        raws = ctx.enter_context(tc.tile_pool(name="raws", bufs=8))
+        x_mids = ctx.enter_context(tc.tile_pool(name="x_mids", bufs=5))
+        w_mids = ctx.enter_context(tc.tile_pool(name="w_mids", bufs=7))
+        ends = ctx.enter_context(tc.tile_pool(name="ends", bufs=2))
         psum = ctx.enter_context(tc.psum_pool(name="psum", bufs=1))
 
         offs_sb = keep.tile([P, SLOTS // 16], U16, name="offs_sb")
@@ -61,87 +58,79 @@ def tile_routed_moe_kernel(tc, xT, w, gate, offs, pos1, pos2, out):
         gates = keep.tile([P, 2, T], F32, name="gates")
         y = keep.tile([P, SLOTS], F32, name="y")
         first = keep.tile([P, T], F32, name="first")
-        second = keep.tile([P, T], F32, name="second")
         warm = keep.tile([P, 8], F32, name="warm")
 
         nc.gpsimd.memset(x_scales[:], 0)
         nc.vector.memset(warm[:], 0.0)
         nc.scalar.copy(warm[:, 4:8], warm[:, 0:4])
 
-        units = [("x",) + u for u in X_UNITS]
-        g0 = 0
-        for size, on_vector, on_gpsimd in W_SIZES:
-            units.append(("w", g0, size, on_vector, on_gpsimd))
-            g0 += size
-        raw_of = {}
-        mid_of = {}
+        loads = []
+        for a, c0, parts in X_UNITS:
+            for n, shares in parts:
+                loads.append(("x", a, c0, n))
+                c0 += n
+        blocks = 0
+        for parts in W_UNITS:
+            for n, shares in parts:
+                loads.append(("w", blocks, n))
+                blocks += n
+        raw_of = []
 
-        def load(u):
-            if u >= len(units):
+        def load(i):
+            if i >= len(loads):
                 return
-            unit = units[u]
-            if unit[0] == "x":
-                kind, a, c0, n, on_vector = unit
+            if loads[i][0] == "x":
+                a, c0, n = loads[i][1:]
                 raw = raws.tile([P, PACK, n], F32, name="raw", tag="raw", align_bytes=64)
                 nc.sync.dma_start(out=raw[:], in_=x_rows[a, :, :, c0:c0 + n])
             else:
-                kind, g, n, on_vector, on_gpsimd = unit
+                g, n = loads[i][1:]
                 raw = raws.tile([P, n, PACK, N], F32, name="raw", tag="raw", align_bytes=64)
                 nc.sync.dma_start(out=raw[:], in_=w_rows[:, g:g + n, :, :])
-            raw_of[u] = raw
-            if u == 1:
+            raw_of.append(raw)
+            if i == 1:
                 nc.sync.dma_start(offs_sb[:], offs)
-            if u == len(units) - 5:
+            if i == len(loads) - 5:
                 nc.sync.dma_start(pos1_sb[:], pos1)
                 nc.sync.dma_start(pos2_sb[:], pos2)
-            if u == len(units) - 1:
+            if i == len(loads) - 1:
                 for r in range(2):
                     nc.sync.dma_start(out=gates[:, r, :], in_=gate[r])
 
-        def interleave(u):
-            unit = units[u]
-            raw = raw_of[u]
-            if unit[0] == "x":
-                kind, a, c0, n, cut = unit
-                mid = mids.tile([P, n, PACK], BF16, name="mid", tag="mid", align_bytes=64)
-                if cut > 0:
-                    dst, src = by_fours(mid[:, 0:cut, :], raw[:, :, 0:cut])
-                    nc.vector.tensor_copy(dst, src)
-                if cut < n:
-                    dst, src = by_fours(mid[:, cut:n, :], raw[:, :, cut:n])
-                    nc.scalar.copy(dst, src)
-            else:
-                kind, g, n, cut, head = unit
-                mid = mids.tile([P, n, N, PACK], BF16, name="mid", tag="mid", align_bytes=64)
-                if cut > 0:
-                    dst, src = by_fours_w(mid[:, n - cut:n], raw[:, n - cut:n])
-                    nc.vector.tensor_copy(dst, src)
-                if head > 0:
-                    dst, src = by_fours_w(mid[:, 0:head], raw[:, 0:head])
-                    nc.gpsimd.tensor_copy(dst, src)
-                if head < n - cut:
-                    dst, src = by_fours_w(mid[:, head:n - cut], raw[:, head:n - cut])
-                    nc.scalar.copy(dst, src)
-            mid_of[u] = mid
+        def interleave_x(mid, at, i, shares):
+            raw = raw_of[i]
+            lo = 0
+            for engine, count in shares:
+                move[engine](
+                    mid[:, at + lo:at + lo + count, :].rearrange("p (c i) t -> p c t i", i=4),
+                    raw[:, :, lo:lo + count].rearrange("p t (c i) -> p c t i", i=4),
+                )
+                lo += count
 
-        def quantize(u):
-            unit = units[u]
-            mid = mid_of[u]
-            if unit[0] == "x":
-                kind, a, c0, n, cut = unit
-                nc.vector.quantize_mx(
-                    out=x_codes[a][:, c0:c0 + n].bitcast(FP8X4),
-                    scales=x_scales[4 * a:P, c0:c0 + n],
-                    in_=mid[:].rearrange("p n t -> p (n t)"),
+        def quantize_x(a, c0, n, mid):
+            nc.vector.quantize_mx(
+                out=x_codes[a][:, c0:c0 + n].bitcast(FP8X4),
+                scales=x_scales[4 * a:P, c0:c0 + n],
+                in_=mid[:].rearrange("p n t -> p (n t)"),
+            )
+
+        def interleave_w(mid, at, i, shares):
+            raw = raw_of[i]
+            lo = 0
+            for engine, count in shares:
+                move[engine](
+                    mid[:, at + lo:at + lo + count].rearrange("p g (c i) t -> p g c t i", i=4),
+                    raw[:, lo:lo + count].rearrange("p g t (c i) -> p g c t i", i=4),
                 )
-            else:
-                kind, g, n, cut, head = unit
-                cols = slice(g * N, (g + n) * N)
-                nc.vector.quantize_mx(
-                    out=w_codes[:, cols].bitcast(FP8X4),
-                    scales=w_scales[:, cols],
-                    in_=mid[:].rearrange("p g n t -> p (g n t)"),
-                )
+                lo += count
+
+        def quantize_w(g, n, mid):
+            cols = slice(g * N, (g + n) * N)
+            nc.vector.quantize_mx(
+                out=w_codes[:, cols].bitcast(FP8X4),
+                scales=w_scales[:, cols],
+                in_=mid[:].rearrange("p g n t -> p (g n t)"),
+            )
 
         def gather_words(a, lo, hi):
             nc.vector.tensor_copy(s_codes[a][:, lo:hi], x_codes[a][:].indirect(offs_sb[:, lo // 16:hi // 16]))
@@ -152,12 +141,12 @@ def tile_routed_moe_kernel(tc, xT, w, gate, offs, pos1, pos2, out):
         bank_of = {}
 
         def multiply(e):
-            for b, (e0, e1) in enumerate(BANKS):
+            for e0, e1 in BANKS:
                 if e0 <= e < e1:
                     break
             if e == e0:
-                bank_of[b] = psum.tile([P, (e1 - e0) * C], F32, name=f"bank{b}")
-            bank = bank_of[b]
+                bank_of[e0] = psum.tile([P, (e1 - e0) * C], F32, name=f"bank{e0}")
+            bank = bank_of[e0]
             for a in range(PASSES):
                 wc = slice((e * PASSES + a) * N, (e * PASSES + a + 1) * N)
                 sc = slice(e * C, (e + 1) * C)
@@ -176,52 +165,82 @@ def tile_routed_moe_kernel(tc, xT, w, gate, offs, pos1, pos2, out):
                 else:
                     nc.scalar.copy(y[:, e0 * C:e1 * C], bank[:])
 
+        for i in range(AHEAD):
+            load(i)
         jobs = []
-        done = 0
 
-        def after(u, done):
-            unit = units[u]
-            if unit[0] == "x":
-                a, last = unit[1], unit[2] + unit[3] == T
-                if last and a < PASSES - 1:
-                    jobs.extend([(gather_words, (a, lo, hi)) for lo, hi in SLOT_CUTS])
-                if last and a == PASSES - 1:
-                    for lo, hi in SLOT_CUTS:
-                        jobs.append((gather_words, (a, lo, hi)))
-                        jobs.append((gather_bytes, (lo, hi)))
-            for i in range(1):
+        def some_jobs(count):
+            for j in range(count):
                 if jobs:
                     f, args = jobs.pop(0)
                     f(*args)
-            if unit[0] == "w" and not jobs:
-                while done < E and (done + 1) * PASSES <= unit[1] + unit[2]:
+
+        i = 0
+        waiting = None
+        for unit in X_UNITS + [None]:
+            if unit is not None:
+                a, c0, parts = unit
+                total = sum(n for n, shares in parts)
+                mid = x_mids.tile([P, total, PACK], BF16, name="x_mid", align_bytes=64)
+                at = 0
+                for n, shares in parts:
+                    interleave_x(mid, at, i, shares)
+                    load(i + AHEAD)
+                    at += n
+                    i += 1
+            if waiting is not None:
+                quantize_x(*waiting)
+                if waiting[1] + waiting[2] == T:
+                    for lo, hi in SLOT_CUTS:
+                        jobs.append((gather_words, (waiting[0], lo, hi)))
+                        if waiting[0] == PASSES - 1:
+                            jobs.append((gather_bytes, (lo, hi)))
+                some_jobs(1)
+            if unit is not None:
+                waiting = (a, c0, total, mid)
+
+        g = 0
+        done = 0
+        waiting = None
+        for parts in W_UNITS + [None]:
+            if parts is not None:
+                total = sum(n for n, shares in parts)
+                mid = w_mids.tile([P, total, N, PACK], BF16, name="w_mid", align_bytes=64)
+                at = 0
+                for n, shares in parts:
+                    interleave_w(mid, at, i, shares)
+                    load(i + AHEAD)
+                    at += n
+                    i += 1
+            if waiting is not None:
+                quantize_w(*waiting)
+                some_jobs(2)
+                while not jobs and done < E and (done + 1) * PASSES <= waiting[0] + waiting[1]:
                     multiply(done)
                     done += 1
-            return done
-
-        for u in range(AHEAD):
-            load(u)
-        for u in range(len(units) + 1):
-            if u < len(units):
-                interleave(u)
-            load(u + AHEAD)
-            if u > 0:
-                quantize(u - 1)
-                done = after(u - 1, done)
+            if parts is not None:
+                waiting = (g, total, mid)
+                g += total
 
         def fetch(dst, r, lo, hi):
             pos = pos1_sb if r == 0 else pos2_sb
-            nc.vector.tensor_tensor(dst[:, lo:hi], y[:].indirect(pos[:, lo // 16:hi // 16]), gates[:, r, lo:hi], MULT)
+            nc.vector.tensor_tensor(dst, y[:].indirect(pos[:, lo // 16:hi // 16]), gates[:, r, lo:hi], MULT)
+
+        second_of = {}
+
+        def fetch_second(lo, hi):
+            second = ends.tile([P, hi - lo], F32, name="second", tag="second")
+            fetch(second[:], 1, lo, hi)
+            second_of[lo] = second
 
         def finish(lo, hi):
-            nc.vector.tensor_add(first[:, lo:hi], first[:, lo:hi], second[:, lo:hi])
+            nc.vector.tensor_add(first[:, lo:hi], first[:, lo:hi], second_of[lo][:])
             nc.sync.dma_start(out=out[:, lo:hi], in_=first[:, lo:hi])
 
-        fetch(first, 0, 0, 512)
-        fetch(first, 0, 512, 1024)
-        fetch(second, 1, 0, 512)
+        fetch(first[:], 0, 0, T)
+        fetch_second(0, 512)
+        fetch_second(512, 896)
         finish(0, 512)
-        fetch(second, 1, 512, 896)
+        fetch_second(896, 1024)
         finish(512, 896)
-        fetch(second, 1, 896, 1024)
         finish(896, 1024)

@@ -21,13 +21,16 @@ AHEAD = 7
 
 
 X_UNITS = [
-    (0, 0, [(512, [("V", 512)])]), (0, 512, [(256, [("S", 256)]), (256, [("V", 256)])]),
+    (0, 0, [(512, [("V", 512)])]), (0, 512, [(256, [("S", 256)])]), (0, 768, [(256, [("V", 128), ("S", 128)])]),
     (1, 0, [(512, [("S", 512)])]), (1, 512, [(512, [("S", 512)])]),
     (2, 0, [(512, [("S", 512)])]), (2, 512, [(512, [("S", 512)])]),
 ]
 W_UNITS = [[(4, [("S", 4)]), (4, [("G", 2), ("S", 2)])]] * 3 + [[(4, [("G", 1), ("S", 3)]), (4, [("G", 2), ("S", 2)])]] * 2 + [
-    [(4, [("G", 1), ("S", 3)])], [(2, [("S", 2)])], [(2, [("S", 1), ("V", 1)])]]
-SLOT_CUTS = [(0, 768), (768, 1408), (1408, 2048)]
+    [(4, [("G", 1), ("S", 3)])], [(2, [("S", 2)])], [(2, [("G", 1), ("S", 1)])]]
+SLOT_CUTS = [(0, 1024), (1024, 2048)]
+LATE_UNIT = 4
+X_JOBS = [[], [], [(0, 0), (0, 1)], [], [(1, 0), (1, 1)], [], [(2, 0), ("b", 0), (2, 1), ("b", 1)]]
+W_JOBS = [[], [], [], [], [], [], [], []]
 BANKS = [(0, 4), (4, 8), (8, 12), (12, 15), (15, 16)]
 
 
@@ -41,7 +44,8 @@ def tile_routed_moe_kernel(tc, xT, w, gate, offs, pos1, pos2, out):
         keep = ctx.enter_context(tc.tile_pool(name="keep", bufs=1))
         raws = ctx.enter_context(tc.tile_pool(name="raws", bufs=8))
         x_mids = ctx.enter_context(tc.tile_pool(name="x_mids", bufs=5))
-        w_mids = ctx.enter_context(tc.tile_pool(name="w_mids", bufs=7))
+        w_mids = ctx.enter_context(tc.tile_pool(name="w_mids", bufs=5))
+        late = ctx.enter_context(tc.tile_pool(name="late", bufs=1))
         ends = ctx.enter_context(tc.tile_pool(name="ends", bufs=2))
         psum = ctx.enter_context(tc.psum_pool(name="psum", bufs=1))
 
@@ -49,18 +53,19 @@ def tile_routed_moe_kernel(tc, xT, w, gate, offs, pos1, pos2, out):
         pos1_sb = keep.tile([P, T // 16], U16, name="pos1_sb")
         pos2_sb = keep.tile([P, T // 16], U16, name="pos2_sb")
 
-        x_codes = [keep.tile([P, T], U32, name=f"x_codes{a}", align_bytes=64) for a in range(PASSES)]
-        x_scales = keep.tile([P, T], U8, name="x_scales", align_bytes=64)
+        x_codes = [keep.tile([P, 2 * T], U32, name=f"x_codes{a}", align_bytes=64) for a in range(PASSES)]
+        x_scales = keep.tile([P, 2 * T], U8, name="x_scales", align_bytes=64)
         s_codes = [keep.tile([P, SLOTS], U32, name=f"s_codes{a}", align_bytes=64) for a in range(PASSES)]
         s_scales = keep.tile([P, SLOTS], U8, name="s_scales", align_bytes=64)
         w_codes = keep.tile([P, E * PASSES * N], U32, name="w_codes", align_bytes=64)
         w_scales = keep.tile([P, E * PASSES * N], U8, name="w_scales", align_bytes=64)
         gates = keep.tile([P, 2, T], F32, name="gates")
-        y = keep.tile([P, SLOTS], F32, name="y")
         first = keep.tile([P, T], F32, name="first")
         warm = keep.tile([P, 8], F32, name="warm")
 
         nc.gpsimd.memset(x_scales[:], 0)
+        for a in range(PASSES):
+            nc.gpsimd.memset(x_codes[a][:, T:].bitcast(mybir.dt.int32), 0)
         nc.vector.memset(warm[:], 0.0)
         nc.scalar.copy(warm[:, 4:8], warm[:, 0:4])
 
@@ -88,7 +93,7 @@ def tile_routed_moe_kernel(tc, xT, w, gate, offs, pos1, pos2, out):
                 raw = raws.tile([P, n, PACK, N], F32, name="raw", tag="raw", align_bytes=64)
                 nc.sync.dma_start(out=raw[:], in_=w_rows[:, g:g + n, :, :])
             raw_of.append(raw)
-            if i == 1:
+            if i == 2:
                 nc.sync.dma_start(offs_sb[:], offs)
             if i == len(loads) - 5:
                 nc.sync.dma_start(pos1_sb[:], pos1)
@@ -140,6 +145,12 @@ def tile_routed_moe_kernel(tc, xT, w, gate, offs, pos1, pos2, out):
 
         bank_of = {}
 
+        def empty(y, e0, e1):
+            if e1 == E:
+                nc.vector.tensor_copy(y[:, e0 * C:e1 * C], bank_of[e0][:])
+            else:
+                nc.scalar.copy(y[:, e0 * C:e1 * C], bank_of[e0][:])
+
         def multiply(e):
             for e0, e1 in BANKS:
                 if e0 <= e < e1:
@@ -159,23 +170,29 @@ def tile_routed_moe_kernel(tc, xT, w, gate, offs, pos1, pos2, out):
                     start=(a == 0),
                     stop=(a == PASSES - 1),
                 )
-            if e == e1 - 1:
-                if e1 == E:
-                    nc.vector.tensor_copy(y[:, e0 * C:e1 * C], bank[:])
-                else:
-                    nc.scalar.copy(y[:, e0 * C:e1 * C], bank[:])
 
         for i in range(AHEAD):
             load(i)
-        jobs = []
+        gathered = set()
 
-        def some_jobs(count):
-            for j in range(count):
-                if jobs:
-                    f, args = jobs.pop(0)
-                    f(*args)
+        def gather(todo):
+            for what, piece in todo:
+                lo, hi = SLOT_CUTS[piece]
+                if what == "b":
+                    gather_bytes(lo, hi)
+                else:
+                    gather_words(what, lo, hi)
+                gathered.add((what, piece))
+
+        def ready(e):
+            for piece, (lo, hi) in enumerate(SLOT_CUTS):
+                if lo < (e + 1) * C and e * C < hi:
+                    if not all((what, piece) in gathered for what in [0, 1, 2, "b"]):
+                        return False
+            return True
 
         i = 0
+        step = 0
         waiting = None
         for unit in X_UNITS + [None]:
             if unit is not None:
@@ -190,22 +207,23 @@ def tile_routed_moe_kernel(tc, xT, w, gate, offs, pos1, pos2, out):
                     i += 1
             if waiting is not None:
                 quantize_x(*waiting)
-                if waiting[1] + waiting[2] == T:
-                    for lo, hi in SLOT_CUTS:
-                        jobs.append((gather_words, (waiting[0], lo, hi)))
-                        if waiting[0] == PASSES - 1:
-                            jobs.append((gather_bytes, (lo, hi)))
-                some_jobs(1)
+                gather(X_JOBS[step])
+                step += 1
             if unit is not None:
                 waiting = (a, c0, total, mid)
 
         g = 0
         done = 0
+        step = 0
+        w_unit = 0
+        y = None
+        emptied = 0
         waiting = None
         for parts in W_UNITS + [None]:
             if parts is not None:
                 total = sum(n for n, shares in parts)
-                mid = w_mids.tile([P, total, N, PACK], BF16, name="w_mid", align_bytes=64)
+                pool = late if w_unit == LATE_UNIT else w_mids
+                mid = pool.tile([P, total, N, PACK], BF16, name="w_mid", tag="w_mid", align_bytes=64)
                 at = 0
                 for n, shares in parts:
                     interleave_w(mid, at, i, shares)
@@ -214,13 +232,21 @@ def tile_routed_moe_kernel(tc, xT, w, gate, offs, pos1, pos2, out):
                     i += 1
             if waiting is not None:
                 quantize_w(*waiting)
-                some_jobs(2)
-                while not jobs and done < E and (done + 1) * PASSES <= waiting[0] + waiting[1]:
+                gather(W_JOBS[step])
+                step += 1
+                while done < E and ready(done) and (done + 1) * PASSES <= waiting[0] + waiting[1]:
                     multiply(done)
                     done += 1
+                if step == LATE_UNIT + 1 or y is not None:
+                    if y is None:
+                        y = late.tile([P, SLOTS], F32, name="y", tag="w_mid", align_bytes=64)
+                    while emptied < len(BANKS) and BANKS[emptied][1] <= done:
+                        empty(y, *BANKS[emptied])
+                        emptied += 1
             if parts is not None:
                 waiting = (g, total, mid)
                 g += total
+                w_unit += 1
 
         def fetch(dst, r, lo, hi):
             pos = pos1_sb if r == 0 else pos2_sb
@@ -238,9 +264,7 @@ def tile_routed_moe_kernel(tc, xT, w, gate, offs, pos1, pos2, out):
             nc.sync.dma_start(out=out[:, lo:hi], in_=first[:, lo:hi])
 
         fetch(first[:], 0, 0, T)
-        fetch_second(0, 512)
-        fetch_second(512, 896)
-        finish(0, 512)
-        fetch_second(896, 1024)
-        finish(512, 896)
-        finish(896, 1024)
+        fetch_second(0, 768)
+        fetch_second(768, 1024)
+        finish(0, 768)
+        finish(768, 1024)

from contextlib import ExitStack

import concourse.mybir as mybir

K, T, E, C, N = 1536, 1024, 16, 128, 128
FLOPS = 2 * K * E * C * N

F32 = mybir.dt.float32
BF16 = mybir.dt.bfloat16
U32 = mybir.dt.uint32
U16 = mybir.dt.uint16
U8 = mybir.dt.uint8
FP8X4 = mybir.dt.float8_e4m3fn_x4
MULT = mybir.AluOpType.mult

P = 128
PACK = 4
PASSES = K // (P * PACK)
SLOTS = E * C
AHEAD = 7


X_UNITS = [
    (0, 0, [(512, [("V", 512)])]), (0, 512, [(256, [("S", 256)])]), (0, 768, [(256, [("V", 128), ("S", 128)])]),
    (1, 0, [(512, [("S", 512)])]), (1, 512, [(512, [("S", 512)])]),
    (2, 0, [(512, [("S", 512)])]), (2, 512, [(512, [("S", 512)])]),
]
W_UNITS = [[(4, [("S", 4)]), (4, [("G", 2), ("S", 2)])]] * 3 + [[(4, [("G", 1), ("S", 3)]), (4, [("G", 2), ("S", 2)])]] * 2 + [
    [(4, [("G", 1), ("S", 3)])], [(2, [("S", 2)])], [(2, [("G", 1), ("S", 1)])]]
SLOT_CUTS = [(0, 1024), (1024, 2048)]
LATE_UNIT = 4
X_JOBS = [[], [], [(0, 0), (0, 1)], [], [(1, 0), (1, 1)], [], [(2, 0), ("b", 0), (2, 1), ("b", 1)]]
W_JOBS = [[], [], [], [], [], [], [], []]
BANKS = [(0, 4), (4, 8), (8, 12), (12, 15), (15, 16)]


def tile_routed_moe_kernel(tc, xT, w, gate, offs, pos1, pos2, out):
    nc = tc.nc
    x_rows = xT.rearrange("(a p t) n -> a p t n", p=P, t=PACK)
    w_rows = w.flatten_outer_dims().rearrange("(g p t) n -> p g t n", p=P, t=PACK)
    move = {"V": nc.vector.tensor_copy, "S": nc.scalar.copy, "G": nc.gpsimd.tensor_copy}

    with ExitStack() as ctx:
        keep = ctx.enter_context(tc.tile_pool(name="keep", bufs=1))
        raws = ctx.enter_context(tc.tile_pool(name="raws", bufs=8))
        x_mids = ctx.enter_context(tc.tile_pool(name="x_mids", bufs=5))
        w_mids = ctx.enter_context(tc.tile_pool(name="w_mids", bufs=5))
        late = ctx.enter_context(tc.tile_pool(name="late", bufs=1))
        ends = ctx.enter_context(tc.tile_pool(name="ends", bufs=2))
        psum = ctx.enter_context(tc.psum_pool(name="psum", bufs=1))

        offs_sb = keep.tile([P, SLOTS // 16], U16, name="offs_sb")
        pos1_sb = keep.tile([P, T // 16], U16, name="pos1_sb")
        pos2_sb = keep.tile([P, T // 16], U16, name="pos2_sb")

        x_codes = [keep.tile([P, 2 * T], U32, name=f"x_codes{a}", align_bytes=64) for a in range(PASSES)]
        x_scales = keep.tile([P, 2 * T], U8, name="x_scales", align_bytes=64)
        s_codes = [keep.tile([P, SLOTS], U32, name=f"s_codes{a}", align_bytes=64) for a in range(PASSES)]
        s_scales = keep.tile([P, SLOTS], U8, name="s_scales", align_bytes=64)
        w_codes = keep.tile([P, E * PASSES * N], U32, name="w_codes", align_bytes=64)
        w_scales = keep.tile([P, E * PASSES * N], U8, name="w_scales", align_bytes=64)
        gates = keep.tile([P, 2, T], F32, name="gates")
        first = keep.tile([P, T], F32, name="first")
        warm = keep.tile([P, 8], F32, name="warm")

        nc.gpsimd.memset(x_scales[:], 0)
        for a in range(PASSES):
            nc.gpsimd.memset(x_codes[a][:, T:].bitcast(mybir.dt.int32), 0)
        nc.vector.memset(warm[:], 0.0)
        nc.scalar.copy(warm[:, 4:8], warm[:, 0:4])

        loads = []
        for a, c0, parts in X_UNITS:
            for n, shares in parts:
                loads.append(("x", a, c0, n))
                c0 += n
        blocks = 0
        for parts in W_UNITS:
            for n, shares in parts:
                loads.append(("w", blocks, n))
                blocks += n
        raw_of = []

        def load(i):
            if i >= len(loads):
                return
            if loads[i][0] == "x":
                a, c0, n = loads[i][1:]
                raw = raws.tile([P, PACK, n], F32, name="raw", tag="raw", align_bytes=64)
                nc.sync.dma_start(out=raw[:], in_=x_rows[a, :, :, c0:c0 + n])
            else:
                g, n = loads[i][1:]
                raw = raws.tile([P, n, PACK, N], F32, name="raw", tag="raw", align_bytes=64)
                nc.sync.dma_start(out=raw[:], in_=w_rows[:, g:g + n, :, :])
            raw_of.append(raw)
            if i == 2:
                nc.sync.dma_start(offs_sb[:], offs)
            if i == len(loads) - 5:
                nc.sync.dma_start(pos1_sb[:], pos1)
                nc.sync.dma_start(pos2_sb[:], pos2)
            if i == len(loads) - 1:
                for r in range(2):
                    nc.sync.dma_start(out=gates[:, r, :], in_=gate[r])

        def interleave_x(mid, at, i, shares):
            raw = raw_of[i]
            lo = 0
            for engine, count in shares:
                move[engine](
                    mid[:, at + lo:at + lo + count, :].rearrange("p (c i) t -> p c t i", i=4),
                    raw[:, :, lo:lo + count].rearrange("p t (c i) -> p c t i", i=4),
                )
                lo += count

        def quantize_x(a, c0, n, mid):
            nc.vector.quantize_mx(
                out=x_codes[a][:, c0:c0 + n].bitcast(FP8X4),
                scales=x_scales[4 * a:P, c0:c0 + n],
                in_=mid[:].rearrange("p n t -> p (n t)"),
            )

        def interleave_w(mid, at, i, shares):
            raw = raw_of[i]
            lo = 0
            for engine, count in shares:
                move[engine](
                    mid[:, at + lo:at + lo + count].rearrange("p g (c i) t -> p g c t i", i=4),
                    raw[:, lo:lo + count].rearrange("p g t (c i) -> p g c t i", i=4),
                )
                lo += count

        def quantize_w(g, n, mid):
            cols = slice(g * N, (g + n) * N)
            nc.vector.quantize_mx(
                out=w_codes[:, cols].bitcast(FP8X4),
                scales=w_scales[:, cols],
                in_=mid[:].rearrange("p g n t -> p (g n t)"),
            )

        def gather_words(a, lo, hi):
            nc.vector.tensor_copy(s_codes[a][:, lo:hi], x_codes[a][:].indirect(offs_sb[:, lo // 16:hi // 16]))

        def gather_bytes(lo, hi):
            nc.vector.tensor_copy(s_scales[:, lo:hi], x_scales[:].indirect(offs_sb[:, lo // 16:hi // 16]))

        bank_of = {}

        def empty(y, e0, e1):
            if e1 == E:
                nc.vector.tensor_copy(y[:, e0 * C:e1 * C], bank_of[e0][:])
            else:
                nc.scalar.copy(y[:, e0 * C:e1 * C], bank_of[e0][:])

        def multiply(e):
            for e0, e1 in BANKS:
                if e0 <= e < e1:
                    break
            if e == e0:
                bank_of[e0] = psum.tile([P, (e1 - e0) * C], F32, name=f"bank{e0}")
            bank = bank_of[e0]
            for a in range(PASSES):
                wc = slice((e * PASSES + a) * N, (e * PASSES + a + 1) * N)
                sc = slice(e * C, (e + 1) * C)
                nc.tensor.matmul_mx(
                    out=bank[:, (e - e0) * C:(e - e0 + 1) * C],
                    lhsT=w_codes[:, wc].bitcast(FP8X4),
                    lhsT_scale=w_scales[:, wc],
                    rhs=s_codes[a][:, sc].bitcast(FP8X4),
                    rhs_scale=s_scales[4 * a:P, sc],
                    start=(a == 0),
                    stop=(a == PASSES - 1),
                )

        for i in range(AHEAD):
            load(i)
        gathered = set()

        def gather(todo):
            for what, piece in todo:
                lo, hi = SLOT_CUTS[piece]
                if what == "b":
                    gather_bytes(lo, hi)
                else:
                    gather_words(what, lo, hi)
                gathered.add((what, piece))

        def ready(e):
            for piece, (lo, hi) in enumerate(SLOT_CUTS):
                if lo < (e + 1) * C and e * C < hi:
                    if not all((what, piece) in gathered for what in [0, 1, 2, "b"]):
                        return False
            return True

        i = 0
        step = 0
        waiting = None
        for unit in X_UNITS + [None]:
            if unit is not None:
                a, c0, parts = unit
                total = sum(n for n, shares in parts)
                mid = x_mids.tile([P, total, PACK], BF16, name="x_mid", align_bytes=64)
                at = 0
                for n, shares in parts:
                    interleave_x(mid, at, i, shares)
                    load(i + AHEAD)
                    at += n
                    i += 1
            if waiting is not None:
                quantize_x(*waiting)
                gather(X_JOBS[step])
                step += 1
            if unit is not None:
                waiting = (a, c0, total, mid)

        g = 0
        done = 0
        step = 0
        w_unit = 0
        y = None
        emptied = 0
        waiting = None
        for parts in W_UNITS + [None]:
            if parts is not None:
                total = sum(n for n, shares in parts)
                pool = late if w_unit == LATE_UNIT else w_mids
                mid = pool.tile([P, total, N, PACK], BF16, name="w_mid", tag="w_mid", align_bytes=64)
                at = 0
                for n, shares in parts:
                    interleave_w(mid, at, i, shares)
                    load(i + AHEAD)
                    at += n
                    i += 1
            if waiting is not None:
                quantize_w(*waiting)
                gather(W_JOBS[step])
                step += 1
                while done < E and ready(done) and (done + 1) * PASSES <= waiting[0] + waiting[1]:
                    multiply(done)
                    done += 1
                if step == LATE_UNIT + 1 or y is not None:
                    if y is None:
                        y = late.tile([P, SLOTS], F32, name="y", tag="w_mid", align_bytes=64)
                    while emptied < len(BANKS) and BANKS[emptied][1] <= done:
                        empty(y, *BANKS[emptied])
                        emptied += 1
            if parts is not None:
                waiting = (g, total, mid)
                g += total
                w_unit += 1

        def fetch(dst, r, lo, hi):
            pos = pos1_sb if r == 0 else pos2_sb
            nc.vector.tensor_tensor(dst, y[:].indirect(pos[:, lo // 16:hi // 16]), gates[:, r, lo:hi], MULT)

        second_of = {}

        def fetch_second(lo, hi):
            second = ends.tile([P, hi - lo], F32, name="second", tag="second")
            fetch(second[:], 1, lo, hi)
            second_of[lo] = second

        def finish(lo, hi):
            nc.vector.tensor_add(first[:, lo:hi], first[:, lo:hi], second_of[lo][:])
            nc.sync.dma_start(out=out[:, lo:hi], in_=first[:, lo:hi])

        fetch(first[:], 0, 0, T)
        fetch_second(0, 768)
        fetch_second(768, 1024)
        finish(0, 768)
        finish(768, 1024)
